import numpy as np
import ml_dtypes


def mxq(x, axis, fmt="e4m3"):
    dtype, down = {"e4m3": (ml_dtypes.float8_e4m3fn, 7), "e5m2": (ml_dtypes.float8_e5m2, 14)}[fmt]
    v = np.moveaxis(np.asarray(x, np.float32).astype(ml_dtypes.bfloat16).astype(np.float64), axis, -1)
    blocks = v.reshape(v.shape[:-1] + (-1, 32))
    amax = np.abs(blocks).max(-1, keepdims=True)
    byte = np.maximum(np.where(amax > 0, np.frexp(amax)[1] - 1 + 127, 0) - down, 1)
    scale = np.exp2(byte - 127.0)
    codes = (blocks / scale).astype(np.float32).astype(dtype).astype(np.float64)
    return np.moveaxis((codes * scale).reshape(v.shape), -1, axis)


WIDE = False


def mx_kscale(k):
    if not WIDE:
        return np.ones(k)
    levels = np.array([10, -10, 5, -5, 0])
    if k % 512:
        return np.exp2(np.random.permutation(np.resize(levels, k // 32))).repeat(32)
    a = np.empty((k // 512, 16))
    for p in range(k // 512):
        a[p, :8] = np.random.permutation(np.resize(levels, 8))
        for g in range(8):
            far = levels[np.abs(levels - a[p, g]) >= 10]
            a[p, g + 8] = far[np.random.randint(len(far))]
    return np.exp2(a.ravel()).repeat(32)


def f64(x):
    return np.asarray(x).astype(np.float64)


def striped8(idx):
    return np.asarray(idx).reshape(8, -1, 16).transpose(0, 2, 1).reshape(128, -1).astype(np.uint16)


def unstriped8(offs):
    return offs.reshape(8, 16, -1).transpose(0, 2, 1).reshape(8, -1).astype(np.int64)


def pick8(x, idx, run):
    r = np.arange(len(x))
    return x[r[:, None], idx[r % (8 * run) // run]]


E2M1 = np.array([0.0, 0.5, 1.0, 1.5, 2.0, 3.0, 4.0, 6.0, -0.0, -0.5, -1.0, -1.5, -2.0, -3.0, -4.0, -6.0])


def pack_weight(w, fmt):
    k, n = w.shape
    w = f64(np.asarray(w, np.float32).astype(ml_dtypes.bfloat16)).reshape(k // 32, 32, n)
    amax = np.abs(w).max(1)
    if fmt == "e4m3":
        byte = np.frexp(amax)[1] - 1 + 127 - 7
    else:
        mant, ex = np.frexp(amax / 6.0)
        byte = np.where(mant > 0.5, ex, ex - 1) + 127
    byte = np.clip(np.where(amax > 0, byte, 1), 1, 254)
    scaled = (w * np.exp2(127.0 - byte)[:, None, :]).reshape(k, n).astype(np.float32)
    by_word = np.ascontiguousarray(scaled.reshape(k // 512, 128, 4, n).transpose(0, 1, 3, 2))
    if fmt == "e4m3":
        words = by_word.astype(ml_dtypes.float8_e4m3fn).view(np.uint8)
    else:
        c = by_word.astype(ml_dtypes.float4_e2m1fn).view(np.uint8) & 0xF
        words = (c[..., 0::2] | (c[..., 1::2] << 4)).reshape(k // 512, 128, 2 * n)
    return np.ascontiguousarray(words), np.ascontiguousarray(byte.astype(np.uint8).reshape(k // 512, 16, n))


def unpack_weight(words, scales, fmt):
    g, _, n = scales.shape
    words = np.ascontiguousarray(words).reshape(g, 128, n, -1)
    if fmt == "e4m3":
        vals = words.view(ml_dtypes.float8_e4m3fn).astype(np.float64)
    else:
        nib = np.empty((g, 128, n, 4), np.uint8)
        nib[..., 0::2] = words & 0xF
        nib[..., 1::2] = words >> 4
        vals = E2M1[nib]
    vals = vals * np.repeat(np.exp2(scales.astype(np.float64) - 127.0), 8, axis=1)[..., None]
    return vals.transpose(0, 1, 3, 2).reshape(g * 512, n)


D, T, U, I, Q = 512, 1024, 1024, 512, 128


def setup_inputs():
    n = np.random.standard_normal
    idx = np.stack([np.random.permutation(T)[:I] for _ in range(8)])
    idx2 = np.stack([np.random.permutation(U)[:I] for _ in range(8)])
    idx3 = np.stack([np.random.permutation(T)[:I] for _ in range(8)])
    idx4 = np.stack([np.random.permutation(U)[:I] for _ in range(8)])
    fd = mx_kscale(D)
    keysp = pack_weight(n((D, T)) / fd[:, None], "e2m1")
    notesp = pack_weight(n((D, U)) / fd[:, None], "e4m3")
    return {
        "query": (n((D, Q)) * 1.0 / np.sqrt(D) * fd[:, None]).astype(np.float32),
        "keys_words": keysp[0],
        "keys_scales": keysp[1],
        "notes_words": notesp[0],
        "notes_scales": notesp[1],
        "offs": striped8(idx),
        "offs2": striped8(idx2),
        "offs3": striped8(idx3),
        "offs4": striped8(idx4),
    }


def reference(query, keys_words, keys_scales, notes_words, notes_scales, offs, offs2, offs3, offs4):
    idx = unstriped8(offs)
    idx2 = unstriped8(offs2)
    idx3 = unstriped8(offs3)
    idx4 = unstriped8(offs4)
    keysu = unpack_weight(keys_words, keys_scales, "e2m1")
    notesu = unpack_weight(notes_words, notes_scales, "e4m3")
    queryq = mxq(f64(query), 0, "e4m3")
    a = queryq.T @ keysu
    b = queryq.T @ notesu
    w = pick8(a, idx, 16) + pick8(b, idx2, 16)
    v = pick8(a, idx3, 16) - pick8(b, idx4, 16)
    f1 = np.zeros((Q, T))
    f1[np.arange(Q)[:, None], idx3[np.arange(Q) % 128 // 16]] = w
    f2 = np.zeros((Q, U))
    f2[np.arange(Q)[:, None], idx2[np.arange(Q) % 128 // 16]] = v
    aa = a - f1
    bb = b + f2
    y = np.maximum(pick8(aa, idx, 16), pick8(bb, idx4, 16))
    return y

@@ -1,0 +1,134 @@
+from contextlib import ExitStack
+
+import concourse.mybir as mybir
+
+F32 = mybir.dt.float32
+BF16 = mybir.dt.bfloat16
+I32 = mybir.dt.int32
+U32 = mybir.dt.uint32
+U16 = mybir.dt.uint16
+U8 = mybir.dt.uint8
+FP8X4 = mybir.dt.float8_e4m3fn_x4
+FP4X4 = mybir.dt.float4_e2m1fn_x4
+ADD = mybir.AluOpType.add
+SUB = mybir.AluOpType.subtract
+MAX = mybir.AluOpType.max
+COPY = mybir.ActivationFunctionType.Copy
+
+P = 128
+PACK = 4
+POOL = 1024
+SLOTS = 512
+HALF = SLOTS // 2
+PIECE = 256
+PIECES = POOL // PIECE
+LIST_COLS = SLOTS // 16
+
+FLOPS = 2 * 2 * 512 * 128 * 1024
+
+
+def tile_attend_crossbook_two_kernel(tc, query, keys_words, keys_scales, notes_words, notes_scales,
+                                      offs, offs2, offs3, offs4, out):
+    nc = tc.nc
+    with ExitStack() as ctx:
+        lists = ctx.enter_context(tc.tile_pool(name="lists", bufs=1))
+        sb = ctx.enter_context(tc.tile_pool(name="sb", bufs=1))
+        psum = ctx.enter_context(tc.psum_pool(name="psum", bufs=1))
+
+        idx1 = lists.tile([P, LIST_COLS], U16, name="idx1")
+        idx2 = lists.tile([P, LIST_COLS], U16, name="idx2")
+        idx3 = lists.tile([P, LIST_COLS], U16, name="idx3")
+        idx4 = lists.tile([P, LIST_COLS], U16, name="idx4")
+
+        q_raw = sb.tile([P, PACK, P], F32, name="q_raw")
+        k_words = sb.tile([P, 2 * POOL], U8, name="k_words", align_bytes=64)
+        k_plane = sb.tile([P, POOL], U8, name="k_plane", align_bytes=64)
+        n_words = sb.tile([P, POOL], I32, name="n_words", align_bytes=64)
+        n_plane = sb.tile([P, POOL], U8, name="n_plane", align_bytes=64)
+        f1 = sb.tile([P, POOL], F32, name="f1")
+        f2 = sb.tile([P, POOL], F32, name="f2")
+
+        nc.vector.memset(k_plane[:].bitcast(I32), 0)
+        nc.vector.memset(n_plane[:].bitcast(I32), 0)
+
+        def load_plane(plane, scales):
+            rows = scales[0].bitcast(I32).rearrange("(Q r) c -> r Q c", r=4)
+            for r in range(4):
+                nc.sync.dma_start(out=plane[:].bitcast(I32)[r:P:32, :], in_=rows[r])
+
+        nc.sync.dma_start(out=q_raw[:], in_=query.rearrange("(p t) q -> p t q", t=PACK))
+        nc.sync.dma_start(out=k_words[:].bitcast(I32), in_=keys_words[0].bitcast(I32))
+        load_plane(k_plane, keys_scales)
+        nc.sync.dma_start(out=n_words[:], in_=notes_words[0].rearrange("p c r -> p (c r)").bitcast(I32))
+        load_plane(n_plane, notes_scales)
+        nc.sync.dma_start(idx1[:], offs)
+        nc.sync.dma_start(idx2[:], offs2)
+        nc.sync.dma_start(idx3[:], offs3)
+        nc.sync.dma_start(idx4[:], offs4)
+
+        nc.vector.memset(f1[:], 0.0)
+        nc.vector.memset(f2[:], 0.0)
+
+        q_bf = sb.tile([P, P, PACK], BF16, name="q_bf", align_bytes=64)
+        q_codes = sb.tile([P, P], U32, name="q_codes", align_bytes=64)
+        q_plane = sb.tile([P, P], U8, name="q_plane", align_bytes=64)
+        nc.vector.tensor_copy(
+            out=q_bf[:].rearrange("p (c i) t -> p c t i", i=4),
+            in_=q_raw[:].rearrange("p t (c i) -> p c t i", i=4))
+        nc.vector.quantize_mx(out=q_codes[:].bitcast(FP8X4), scales=q_plane[:],
+                              in_=q_bf[:].rearrange("p q t -> p (q t)"))
+
+        a = sb.tile([P, POOL], F32, name="a")
+        b = sb.tile([P, POOL], F32, name="b")
+        for j in range(PIECES):
+            cols = slice(j * PIECE, (j + 1) * PIECE)
+            bank = psum.tile([P, PIECE], F32, name="a_bank%d" % j)
+            nc.tensor.matmul_mx(out=bank[:], lhsT=q_codes[:].bitcast(FP8X4), lhsT_scale=q_plane[:],
+                                rhs=k_words[:, 2 * j * PIECE: 2 * (j + 1) * PIECE].bitcast(FP4X4),
+                                rhs_scale=k_plane[:, cols], start=True, stop=True)
+            if j % 2 == 0:
+                nc.scalar.copy(out=a[:, cols], in_=bank[:])
+            else:
+                nc.vector.tensor_copy(out=a[:, cols], in_=bank[:])
+        for j in range(PIECES):
+            cols = slice(j * PIECE, (j + 1) * PIECE)
+            bank = psum.tile([P, PIECE], F32, name="b_bank%d" % j)
+            nc.tensor.matmul_mx(out=bank[:], lhsT=q_codes[:].bitcast(FP8X4), lhsT_scale=q_plane[:],
+                                rhs=n_words[:, cols].bitcast(FP8X4),
+                                rhs_scale=n_plane[:, cols], start=True, stop=True)
+            nc.vector.tensor_copy(out=b[:, cols], in_=bank[:])
+
+        lo_offs, hi_offs = slice(0, LIST_COLS // 2), slice(LIST_COLS // 2, LIST_COLS)
+        lo, hi = slice(0, HALF), slice(HALF, SLOTS)
+
+        a1 = sb.tile([P, SLOTS], F32, name="a1")
+        b2_lo = sb.tile([P, HALF], F32, name="b2_lo")
+        b2_hi = sb.tile([P, HALF], F32, name="b2_hi")
+        a3 = sb.tile([P, SLOTS], F32, name="a3")
+        b4_neg = sb.tile([P, SLOTS], F32, name="b4_neg")
+        nc.scalar.activation(a1[:], a[:].indirect(idx1[:]), COPY)
+        nc.vector.tensor_copy(b2_lo[:], b[:].indirect(idx2[:, lo_offs]))
+        nc.scalar.activation(b2_hi[:], b[:].indirect(idx2[:, hi_offs]), COPY)
+        nc.vector.tensor_tensor(f1[:].indirect(idx3[:, lo_offs]), a1[:, lo], b2_lo[:], ADD)
+        nc.vector.tensor_tensor(f1[:].indirect(idx3[:, hi_offs]), a1[:, hi], b2_hi[:], ADD)
+        nc.scalar.activation(a3[:], a[:].indirect(idx3[:]), COPY)
+        nc.scalar.activation(b4_neg[:], b[:].indirect(idx4[:]), COPY, scale=-1.0)
+
+        aa = sb.tile([P, POOL], F32, name="aa")
+        bb = sb.tile([P, POOL], F32, name="bb")
+        aa1 = sb.tile([P, SLOTS], F32, name="aa1")
+        nc.vector.tensor_tensor(aa[:], a[:], f1[:], SUB)
+        nc.scalar.activation(aa1[:], aa[:].indirect(idx1[:]), COPY)
+        nc.vector.tensor_tensor(f2[:].indirect(idx2[:]), a3[:], b4_neg[:], ADD)
+        nc.vector.tensor_tensor(bb[:], b[:], f2[:], ADD)
+
+        bb4_lo = sb.tile([P, HALF], F32, name="bb4_lo")
+        bb4_hi = sb.tile([P, HALF], F32, name="bb4_hi")
+        y_lo = sb.tile([P, HALF], F32, name="y_lo")
+        y_hi = sb.tile([P, HALF], F32, name="y_hi")
+        nc.vector.tensor_copy(bb4_lo[:], bb[:].indirect(idx4[:, lo_offs]))
+        nc.scalar.activation(bb4_hi[:], bb[:].indirect(idx4[:, hi_offs]), COPY)
+        nc.vector.tensor_tensor(y_lo[:], aa1[:, lo], bb4_lo[:], MAX)
+        nc.sync.dma_start(out=out[:, lo], in_=y_lo[:])
+        nc.vector.tensor_tensor(y_hi[:], aa1[:, hi], bb4_hi[:], MAX)
+        nc.scalar.dma_start(out=out[:, hi], in_=y_hi[:])

@@ -23,6 +23,7 @@ HALF = SLOTS // 2
 PIECE = 256
 PIECES = POOL // PIECE
 LIST_COLS = SLOTS // 16
+BB_SPLIT = 704
 
 FLOPS = 2 * 2 * 512 * 128 * 1024
 
@@ -90,9 +91,11 @@ def tile_attend_crossbook_two_kernel(tc, query, keys_words, keys_scales, notes_w
                 nc.scalar.copy(out=a[:, cols], in_=bank[:])
             else:
                 nc.vector.tensor_copy(out=a[:, cols], in_=bank[:])
+        b_banks = []
         for j in range(PIECES):
             cols = slice(j * PIECE, (j + 1) * PIECE)
             bank = psum.tile([P, PIECE], F32, name="b_bank%d" % j)
+            b_banks.append(bank)
             nc.tensor.matmul_mx(out=bank[:], lhsT=q_codes[:].bitcast(FP8X4), lhsT_scale=q_plane[:],
                                 rhs=n_words[:, cols].bitcast(FP8X4),
                                 rhs_scale=n_plane[:, cols], start=True, stop=True)
@@ -101,26 +104,38 @@ def tile_attend_crossbook_two_kernel(tc, query, keys_words, keys_scales, notes_w
         lo_offs, hi_offs = slice(0, LIST_COLS // 2), slice(LIST_COLS // 2, LIST_COLS)
         lo, hi = slice(0, HALF), slice(HALF, SLOTS)
 
-        a1 = sb.tile([P, SLOTS], F32, name="a1")
-        b2_lo = sb.tile([P, HALF], F32, name="b2_lo")
+        a1_lo = sb.tile([P, HALF], F32, name="a1_lo")
+        a1_hi = sb.tile([P, HALF], F32, name="a1_hi")
         b2_hi = sb.tile([P, HALF], F32, name="b2_hi")
+        w_lo = sb.tile([P, HALF], F32, name="w_lo")
+        w_hi = sb.tile([P, HALF], F32, name="w_hi")
         a3 = sb.tile([P, SLOTS], F32, name="a3")
-        b4_neg = sb.tile([P, SLOTS], F32, name="b4_neg")
-        nc.scalar.activation(a1[:], a[:].indirect(idx1[:]), COPY)
-        nc.vector.tensor_copy(b2_lo[:], b[:].indirect(idx2[:, lo_offs]))
+        b4_lo = sb.tile([P, HALF], F32, name="b4_lo")
+        b4_hi = sb.tile([P, HALF], F32, name="b4_hi", tag="b4_hi_then_aa")
+        v = sb.tile([P, SLOTS], F32, name="v")
+        nc.scalar.activation(a1_lo[:], a[:].indirect(idx1[:, lo_offs]), COPY)
+        nc.scalar.activation(a1_hi[:], a[:].indirect(idx1[:, hi_offs]), COPY)
+        nc.vector.tensor_tensor(w_lo[:], b[:].indirect(idx2[:, lo_offs]), a1_lo[:], ADD)
         nc.scalar.activation(b2_hi[:], b[:].indirect(idx2[:, hi_offs]), COPY)
-        nc.vector.tensor_tensor(f1[:].indirect(idx3[:, lo_offs]), a1[:, lo], b2_lo[:], ADD)
-        nc.vector.tensor_tensor(f1[:].indirect(idx3[:, hi_offs]), a1[:, hi], b2_hi[:], ADD)
+        nc.gpsimd.tensor_tensor(w_hi[:], a1_hi[:], b2_hi[:], ADD)
+        nc.vector.tensor_copy(f1[:].indirect(idx3[:, lo_offs]), w_lo[:])
+        nc.vector.tensor_copy(f1[:].indirect(idx3[:, hi_offs]), w_hi[:])
         nc.scalar.activation(a3[:], a[:].indirect(idx3[:]), COPY)
-        nc.scalar.activation(b4_neg[:], b[:].indirect(idx4[:]), COPY, scale=-1.0)
+        nc.scalar.activation(b4_lo[:], b[:].indirect(idx4[:, lo_offs]), COPY)
+        nc.gpsimd.tensor_tensor(v[:, lo], a3[:, lo], b4_lo[:], SUB)
+        nc.scalar.activation(b4_hi[:], b[:].indirect(idx4[:, hi_offs]), COPY)
+        nc.gpsimd.tensor_tensor(v[:, hi], a3[:, hi], b4_hi[:], SUB)
 
-        aa = sb.tile([P, POOL], F32, name="aa")
+        aa = sb.tile([P, POOL], F32, name="aa", tag="b4_hi_then_aa")
         bb = sb.tile([P, POOL], F32, name="bb")
         aa1 = sb.tile([P, SLOTS], F32, name="aa1")
-        nc.vector.tensor_tensor(aa[:], a[:], f1[:], SUB)
+        nc.vector.tensor_copy(f2[:].indirect(idx2[:]), v[:])
+        nc.gpsimd.tensor_tensor(aa[:], a[:], f1[:], SUB)
         nc.scalar.activation(aa1[:], aa[:].indirect(idx1[:]), COPY)
-        nc.vector.tensor_tensor(f2[:].indirect(idx2[:]), a3[:], b4_neg[:], ADD)
-        nc.vector.tensor_tensor(bb[:], b[:], f2[:], ADD)
+        nc.gpsimd.tensor_tensor(bb[:, BB_SPLIT:], b[:, BB_SPLIT:], f2[:, BB_SPLIT:], ADD)
+        for c0 in range(0, BB_SPLIT, PIECE):
+            c1 = min(c0 + PIECE, BB_SPLIT)
+            nc.vector.tensor_tensor(bb[:, c0:c1], b_banks[c0 // PIECE][:, : c1 - c0], f2[:, c0:c1], ADD)
 
         bb4_lo = sb.tile([P, HALF], F32, name="bb4_lo")
         bb4_hi = sb.tile([P, HALF], F32, name="bb4_hi")

from contextlib import ExitStack

import concourse.mybir as mybir

F32 = mybir.dt.float32
BF16 = mybir.dt.bfloat16
I32 = mybir.dt.int32
U32 = mybir.dt.uint32
U16 = mybir.dt.uint16
U8 = mybir.dt.uint8
FP8X4 = mybir.dt.float8_e4m3fn_x4
FP4X4 = mybir.dt.float4_e2m1fn_x4
ADD = mybir.AluOpType.add
SUB = mybir.AluOpType.subtract
MAX = mybir.AluOpType.max
COPY = mybir.ActivationFunctionType.Copy

P = 128
PACK = 4
POOL = 1024
SLOTS = 512
HALF = SLOTS // 2
PIECE = 256
PIECES = POOL // PIECE
LIST_COLS = SLOTS // 16
BB_SPLIT = 704

FLOPS = 2 * 2 * 512 * 128 * 1024


def tile_attend_crossbook_two_kernel(tc, query, keys_words, keys_scales, notes_words, notes_scales,
                                      offs, offs2, offs3, offs4, out):
    nc = tc.nc
    with ExitStack() as ctx:
        lists = ctx.enter_context(tc.tile_pool(name="lists", bufs=1))
        sb = ctx.enter_context(tc.tile_pool(name="sb", bufs=1))
        psum = ctx.enter_context(tc.psum_pool(name="psum", bufs=1))

        idx1 = lists.tile([P, LIST_COLS], U16, name="idx1")
        idx2 = lists.tile([P, LIST_COLS], U16, name="idx2")
        idx3 = lists.tile([P, LIST_COLS], U16, name="idx3")
        idx4 = lists.tile([P, LIST_COLS], U16, name="idx4")

        q_raw = sb.tile([P, PACK, P], F32, name="q_raw")
        k_words = sb.tile([P, 2 * POOL], U8, name="k_words", align_bytes=64)
        k_plane = sb.tile([P, POOL], U8, name="k_plane", align_bytes=64)
        n_words = sb.tile([P, POOL], I32, name="n_words", align_bytes=64)
        n_plane = sb.tile([P, POOL], U8, name="n_plane", align_bytes=64)
        f1 = sb.tile([P, POOL], F32, name="f1")
        f2 = sb.tile([P, POOL], F32, name="f2")

        nc.vector.memset(k_plane[:].bitcast(I32), 0)
        nc.vector.memset(n_plane[:].bitcast(I32), 0)

        def load_plane(plane, scales):
            rows = scales[0].bitcast(I32).rearrange("(Q r) c -> r Q c", r=4)
            for r in range(4):
                nc.sync.dma_start(out=plane[:].bitcast(I32)[r:P:32, :], in_=rows[r])

        nc.sync.dma_start(out=q_raw[:], in_=query.rearrange("(p t) q -> p t q", t=PACK))
        nc.sync.dma_start(out=k_words[:].bitcast(I32), in_=keys_words[0].bitcast(I32))
        load_plane(k_plane, keys_scales)
        nc.sync.dma_start(out=n_words[:], in_=notes_words[0].rearrange("p c r -> p (c r)").bitcast(I32))
        load_plane(n_plane, notes_scales)
        nc.sync.dma_start(idx1[:], offs)
        nc.sync.dma_start(idx2[:], offs2)
        nc.sync.dma_start(idx3[:], offs3)
        nc.sync.dma_start(idx4[:], offs4)

        nc.vector.memset(f1[:], 0.0)
        nc.vector.memset(f2[:], 0.0)

        q_bf = sb.tile([P, P, PACK], BF16, name="q_bf", align_bytes=64)
        q_codes = sb.tile([P, P], U32, name="q_codes", align_bytes=64)
        q_plane = sb.tile([P, P], U8, name="q_plane", align_bytes=64)
        nc.vector.tensor_copy(
            out=q_bf[:].rearrange("p (c i) t -> p c t i", i=4),
            in_=q_raw[:].rearrange("p t (c i) -> p c t i", i=4))
        nc.vector.quantize_mx(out=q_codes[:].bitcast(FP8X4), scales=q_plane[:],
                              in_=q_bf[:].rearrange("p q t -> p (q t)"))

        a = sb.tile([P, POOL], F32, name="a")
        b = sb.tile([P, POOL], F32, name="b")
        for j in range(PIECES):
            cols = slice(j * PIECE, (j + 1) * PIECE)
            bank = psum.tile([P, PIECE], F32, name="a_bank%d" % j)
            nc.tensor.matmul_mx(out=bank[:], lhsT=q_codes[:].bitcast(FP8X4), lhsT_scale=q_plane[:],
                                rhs=k_words[:, 2 * j * PIECE: 2 * (j + 1) * PIECE].bitcast(FP4X4),
                                rhs_scale=k_plane[:, cols], start=True, stop=True)
            if j % 2 == 0:
                nc.scalar.copy(out=a[:, cols], in_=bank[:])
            else:
                nc.vector.tensor_copy(out=a[:, cols], in_=bank[:])
        b_banks = []
        for j in range(PIECES):
            cols = slice(j * PIECE, (j + 1) * PIECE)
            bank = psum.tile([P, PIECE], F32, name="b_bank%d" % j)
            b_banks.append(bank)
            nc.tensor.matmul_mx(out=bank[:], lhsT=q_codes[:].bitcast(FP8X4), lhsT_scale=q_plane[:],
                                rhs=n_words[:, cols].bitcast(FP8X4),
                                rhs_scale=n_plane[:, cols], start=True, stop=True)
            nc.vector.tensor_copy(out=b[:, cols], in_=bank[:])

        lo_offs, hi_offs = slice(0, LIST_COLS // 2), slice(LIST_COLS // 2, LIST_COLS)
        lo, hi = slice(0, HALF), slice(HALF, SLOTS)

        a1_lo = sb.tile([P, HALF], F32, name="a1_lo")
        a1_hi = sb.tile([P, HALF], F32, name="a1_hi")
        b2_hi = sb.tile([P, HALF], F32, name="b2_hi")
        w_lo = sb.tile([P, HALF], F32, name="w_lo")
        w_hi = sb.tile([P, HALF], F32, name="w_hi")
        a3 = sb.tile([P, SLOTS], F32, name="a3")
        b4_lo = sb.tile([P, HALF], F32, name="b4_lo")
        b4_hi = sb.tile([P, HALF], F32, name="b4_hi", tag="b4_hi_then_aa")
        v = sb.tile([P, SLOTS], F32, name="v")
        nc.scalar.activation(a1_lo[:], a[:].indirect(idx1[:, lo_offs]), COPY)
        nc.scalar.activation(a1_hi[:], a[:].indirect(idx1[:, hi_offs]), COPY)
        nc.vector.tensor_tensor(w_lo[:], b[:].indirect(idx2[:, lo_offs]), a1_lo[:], ADD)
        nc.scalar.activation(b2_hi[:], b[:].indirect(idx2[:, hi_offs]), COPY)
        nc.gpsimd.tensor_tensor(w_hi[:], a1_hi[:], b2_hi[:], ADD)
        nc.vector.tensor_copy(f1[:].indirect(idx3[:, lo_offs]), w_lo[:])
        nc.vector.tensor_copy(f1[:].indirect(idx3[:, hi_offs]), w_hi[:])
        nc.scalar.activation(a3[:], a[:].indirect(idx3[:]), COPY)
        nc.scalar.activation(b4_lo[:], b[:].indirect(idx4[:, lo_offs]), COPY)
        nc.gpsimd.tensor_tensor(v[:, lo], a3[:, lo], b4_lo[:], SUB)
        nc.scalar.activation(b4_hi[:], b[:].indirect(idx4[:, hi_offs]), COPY)
        nc.gpsimd.tensor_tensor(v[:, hi], a3[:, hi], b4_hi[:], SUB)

        aa = sb.tile([P, POOL], F32, name="aa", tag="b4_hi_then_aa")
        bb = sb.tile([P, POOL], F32, name="bb")
        aa1 = sb.tile([P, SLOTS], F32, name="aa1")
        nc.vector.tensor_copy(f2[:].indirect(idx2[:]), v[:])
        nc.gpsimd.tensor_tensor(aa[:], a[:], f1[:], SUB)
        nc.scalar.activation(aa1[:], aa[:].indirect(idx1[:]), COPY)
        nc.gpsimd.tensor_tensor(bb[:, BB_SPLIT:], b[:, BB_SPLIT:], f2[:, BB_SPLIT:], ADD)
        for c0 in range(0, BB_SPLIT, PIECE):
            c1 = min(c0 + PIECE, BB_SPLIT)
            nc.vector.tensor_tensor(bb[:, c0:c1], b_banks[c0 // PIECE][:, : c1 - c0], f2[:, c0:c1], ADD)

        bb4_lo = sb.tile([P, HALF], F32, name="bb4_lo")
        bb4_hi = sb.tile([P, HALF], F32, name="bb4_hi")
        y_lo = sb.tile([P, HALF], F32, name="y_lo")
        y_hi = sb.tile([P, HALF], F32, name="y_hi")
        nc.vector.tensor_copy(bb4_lo[:], bb[:].indirect(idx4[:, lo_offs]))
        nc.scalar.activation(bb4_hi[:], bb[:].indirect(idx4[:, hi_offs]), COPY)
        nc.vector.tensor_tensor(y_lo[:], aa1[:, lo], bb4_lo[:], MAX)
        nc.sync.dma_start(out=out[:, lo], in_=y_lo[:])
        nc.vector.tensor_tensor(y_hi[:], aa1[:, hi], bb4_hi[:], MAX)
        nc.scalar.dma_start(out=out[:, hi], in_=y_hi[:])
